import numpy as np
import ml_dtypes


def mxq(x, axis, fmt="e4m3"):
    dtype, down = {"e4m3": (ml_dtypes.float8_e4m3fn, 7), "e5m2": (ml_dtypes.float8_e5m2, 14)}[fmt]
    v = np.moveaxis(np.asarray(x, np.float32).astype(ml_dtypes.bfloat16).astype(np.float64), axis, -1)
    blocks = v.reshape(v.shape[:-1] + (-1, 32))
    amax = np.abs(blocks).max(-1, keepdims=True)
    byte = np.maximum(np.where(amax > 0, np.frexp(amax)[1] - 1 + 127, 0) - down, 1)
    scale = np.exp2(byte - 127.0)
    codes = (blocks / scale).astype(np.float32).astype(dtype).astype(np.float64)
    return np.moveaxis((codes * scale).reshape(v.shape), -1, axis)


WIDE = False


def mx_kscale(k):
    if not WIDE:
        return np.ones(k)
    levels = np.array([10, -10, 5, -5, 0])
    if k % 512:
        return np.exp2(np.random.permutation(np.resize(levels, k // 32))).repeat(32)
    a = np.empty((k // 512, 16))
    for p in range(k // 512):
        a[p, :8] = np.random.permutation(np.resize(levels, 8))
        for g in range(8):
            far = levels[np.abs(levels - a[p, g]) >= 10]
            a[p, g + 8] = far[np.random.randint(len(far))]
    return np.exp2(a.ravel()).repeat(32)


def f64(x):
    return np.asarray(x).astype(np.float64)


def striped(idx):
    return np.tile(idx.reshape(-1, 16).T, (8, 1)).astype(np.uint16)


def unstriped(offs):
    return offs[:16].T.reshape(-1).astype(np.int64)


E2M1 = np.array([0.0, 0.5, 1.0, 1.5, 2.0, 3.0, 4.0, 6.0, -0.0, -0.5, -1.0, -1.5, -2.0, -3.0, -4.0, -6.0])


def pack_weight(w, fmt):
    k, n = w.shape
    w = f64(np.asarray(w, np.float32).astype(ml_dtypes.bfloat16)).reshape(k // 32, 32, n)
    amax = np.abs(w).max(1)
    if fmt == "e4m3":
        byte = np.frexp(amax)[1] - 1 + 127 - 7
    else:
        mant, ex = np.frexp(amax / 6.0)
        byte = np.where(mant > 0.5, ex, ex - 1) + 127
    byte = np.clip(np.where(amax > 0, byte, 1), 1, 254)
    scaled = (w * np.exp2(127.0 - byte)[:, None, :]).reshape(k, n).astype(np.float32)
    by_word = np.ascontiguousarray(scaled.reshape(k // 512, 128, 4, n).transpose(0, 1, 3, 2))
    if fmt == "e4m3":
        words = by_word.astype(ml_dtypes.float8_e4m3fn).view(np.uint8)
    else:
        c = by_word.astype(ml_dtypes.float4_e2m1fn).view(np.uint8) & 0xF
        words = (c[..., 0::2] | (c[..., 1::2] << 4)).reshape(k // 512, 128, 2 * n)
    return np.ascontiguousarray(words), np.ascontiguousarray(byte.astype(np.uint8).reshape(k // 512, 16, n))


def unpack_weight(words, scales, fmt):
    g, _, n = scales.shape
    words = np.ascontiguousarray(words).reshape(g, 128, n, -1)
    if fmt == "e4m3":
        vals = words.view(ml_dtypes.float8_e4m3fn).astype(np.float64)
    else:
        nib = np.empty((g, 128, n, 4), np.uint8)
        nib[..., 0::2] = words & 0xF
        nib[..., 1::2] = words >> 4
        vals = E2M1[nib]
    vals = vals * np.repeat(np.exp2(scales.astype(np.float64) - 127.0), 8, axis=1)[..., None]
    return vals.transpose(0, 1, 3, 2).reshape(g * 512, n)


def gelu(v):
    return 0.5 * v * (1.0 + np.tanh(np.sqrt(2.0 / np.pi) * (v + 0.044715 * v**3)))


K, T, H, S, S2, T3, P = 1024, 4096, 512, 1024, 1024, 2048, 512

def setup_inputs():
    n = np.random.standard_normal
    s = mx_kscale(K)[:, None]
    u = mx_kscale(H)[:, None]
    d = {}
    d["tab_words"], d["tab_scales"] = pack_weight(n((K, T)) * s, "e4m3")
    d["offs"] = striped(np.random.permutation(T)[:S])
    d["tab2_words"], d["tab2_scales"] = pack_weight(n((H, T3)) / H ** 0.5 / u, "e4m3")
    d["offs2"] = striped(np.random.permutation(T3)[:S2])
    d["pos1"] = striped(np.random.permutation(S)[:P])
    d["pos2"] = striped(np.random.permutation(S)[:P])
    d["w1_words"], d["w1_scales"] = pack_weight(0.34 * n((K, H)) / K ** 0.5 / s, "e2m1")
    d["w2"] = (n((K, H)) / K ** 0.5 / s * u.T).astype(np.float32)
    d["w3"] = (0.7 * n((K, H)) / K ** 0.5 / s * u.T).astype(np.float32)
    d["phase"] = np.random.uniform(-1.0, 1.0, H).astype(np.float32)
    d["music"] = np.exp(0.4 * n((S2, P))).astype(np.float32)
    return d

def reference(tab_words, tab_scales, offs, tab2_words, tab2_scales, offs2, pos1, pos2,
              w1_words, w1_scales, w2, w3, phase, music):
    v = unpack_weight(tab_words, tab_scales, "e4m3")[:, unstriped(offs)]
    v2 = unpack_weight(tab2_words, tab2_scales, "e4m3")[:, unstriped(offs2)]
    w1 = unpack_weight(w1_words, w1_scales, "e2m1")
    angle = (w1.T @ v) + f64(phase)[:, None]
    motif = mxq(f64(w2), 0, "e4m3").T @ v
    kept = mxq(f64(w3), 0, "e4m3").T @ v
    h = np.cos(angle) * motif + kept
    e = v2.T @ mxq(h, 0, "e4m3")
    lead = e[:, unstriped(pos1)]
    partner = e[:, unstriped(pos2)]
    return lead * partner * f64(music)

import math
from contextlib import ExitStack

import concourse.mybir as mybir

F32 = mybir.dt.float32
BF16 = mybir.dt.bfloat16
I32 = mybir.dt.int32
U32 = mybir.dt.uint32
U16 = mybir.dt.uint16
U8 = mybir.dt.uint8
FP8X4 = mybir.dt.float8_e4m3fn_x4
FP4X4 = mybir.dt.float4_e2m1fn_x4
ALU = mybir.AluOpType
ACT = mybir.ActivationFunctionType

K, T, H, S, S2, T3, NP = 1024, 4096, 512, 1024, 1024, 2048, 512
FLOPS = 2 * (3 * K * H * S + H * S2 * S)
P = 128
PASSES = K // 512
HALF = 512
SLOT = 8192
TWO_PI = 2.0 * math.pi


def tile_list_choreology_fragment_pairs_kernel(
    tc, tab_words, tab_scales, offs, tab2_words, tab2_scales, offs2, pos1, pos2,
    w1_words, w1_scales, w2, w3, phase, music, out,
):
    nc = tc.nc
    with ExitStack() as ctx:
        keep = ctx.enter_context(tc.tile_pool(name="keep", bufs=1))
        ring = ctx.enter_context(tc.tile_pool(name="ring", bufs=3))
        big = ctx.enter_context(tc.tile_pool(name="big", bufs=1))
        psum = ctx.enter_context(tc.psum_pool(name="psum", bufs=8))

        def kept_tile(shape, dtype, name):
            return keep.tile(shape, dtype, name=name, align_bytes=64)

        idx = kept_tile([P, S // 16], U16, "idx")
        idx2 = kept_tile([P, S2 // 16], U16, "idx2")
        p1 = kept_tile([P, NP // 16], U16, "p1")
        p2 = kept_tile([P, NP // 16], U16, "p2")
        tab_w = [big.tile([P, T], I32, name="tab_w%d" % a, offset=2 * SLOT * a, align_bytes=64) for a in range(PASSES)]
        tab_s = big.tile([P, T], U8, name="tab_s", offset=SLOT * 5, align_bytes=64)
        tab2_s = kept_tile([P, T3], U8, "tab2_s")
        w1_raw = kept_tile([P, PASSES * H * 2], U8, "w1_raw")
        w1s_raw = kept_tile([P, PASSES * H], U8, "w1s_raw")
        w1_c = kept_tile([P, PASSES * H * 2], U8, "w1_c")
        v_s = kept_tile([P, S], U8, "v_s")
        v_s1 = kept_tile([P, S], U8, "v_s1")
        ph = kept_tile([P, 4], F32, "ph")
        ph_turns = kept_tile([P, 4], F32, "ph_turns")
        warm = kept_tile([P, 1], F32, "warm")

        nc.gpsimd.memset(tab_s[:, : T // 2].bitcast(I32), 0)
        nc.vector.memset(tab_s[:, T // 2 :].bitcast(I32), 0)
        nc.vector.memset(w1s_raw[:].bitcast(I32), 0)
        nc.gpsimd.memset(tab2_s[:].bitcast(I32), 0)
        nc.vector.memset(v_s1[:].bitcast(I32), 0)
        nc.vector.memset(warm[:], 0.0)

        w_raw = {}

        def load_w(name, w, a, offset):
            w_raw[name, a] = big.tile([P, 4, H], F32, name="%s_raw%d" % (name, a), offset=offset, align_bytes=64)
            nc.sync.dma_start(w_raw[name, a][:], w[512 * a : 512 * (a + 1), :].rearrange("(p j) c -> p j c", j=4))

        def load_tab(a, cols):
            nc.sync.dma_start(tab_w[a][:, cols], tab_words[a].rearrange("p n i -> p (n i)").bitcast(I32)[:, cols])

        nc.sync.dma_start(idx[:], offs)
        load_tab(0, slice(0, T // 2))
        nc.sync.dma_start(w1_raw[:].bitcast(I32).rearrange("p (a c) -> p a c", a=PASSES),
                          w1_words.bitcast(I32).rearrange("a p c -> p a c"))
        for q in range(4):
            nc.sync.dma_start(tab_s[32 * q : 32 * q + 8, :].bitcast(I32),
                              tab_scales[:, 4 * q : 4 * q + 4, :].bitcast(I32))
        for q in range(4):
            nc.scalar.dma_start(w1s_raw[32 * q : 32 * q + 4, :].bitcast(I32).rearrange("r (a c) -> r a c", a=PASSES),
                                w1_scales[:, 4 * q : 4 * q + 4, :].bitcast(I32).rearrange("a r c -> r a c"))
        load_tab(0, slice(T // 2, T))
        load_tab(1, slice(0, T))
        nc.sync.dma_start(ph[:], phase.rearrange("(p t) -> p t", t=4))
        nc.sync.dma_start(idx2[:], offs2)
        nc.sync.dma_start(p1[:], pos1)
        nc.sync.dma_start(p2[:], pos2)
        for q in range(4):
            nc.gpsimd.dma_start(tab2_s[32 * q : 32 * q + 4, :].bitcast(I32),
                                tab2_scales[0, 4 * q : 4 * q + 4, :].bitcast(I32))
        nc.scalar.activation(warm[:], warm[:], ACT.Sin)

        nc.vector.tensor_copy(v_s[:], tab_s[:].indirect(idx[:]))
        for q in range(4):
            nc.scalar.dma_start(v_s1[32 * q : 32 * q + 4, :].bitcast(I32), v_s[32 * q + 4 : 32 * q + 8, :].bitcast(I32))
        v_planes = [v_s, v_s1]
        w1_s = kept_tile([P, PASSES * H], U8, "w1_s")
        nc.vector.tensor_copy(
            w1_c[:].bitcast(U16).rearrange("p (a t m) -> p a m t", a=PASSES, t=4),
            w1_raw[:].bitcast(U16).rearrange("p (a m t) -> p a m t", a=PASSES, t=4))
        nc.vector.tensor_copy(
            w1_s[:].rearrange("p (a t m) -> p a m t", a=PASSES, t=4),
            w1s_raw[:].rearrange("p (a m t) -> p a m t", a=PASSES, t=4))
        nc.vector.tensor_scalar(ph_turns[:], ph[:], 1.0 / TWO_PI, None, ALU.mult)
        v_c = {}
        for a in range(PASSES):
            for hf in range(2):
                if (a, hf) == (0, 1):
                    v_c[a, hf] = big.tile([P, HALF], U32, name="v_c01", offset=SLOT * 5, align_bytes=64)
                else:
                    v_c[a, hf] = kept_tile([P, HALF], U32, "v_c%d%d" % (a, hf))
                nc.vector.tensor_copy(v_c[a, hf][:], tab_w[a][:].bitcast(U32).indirect(idx[:, 32 * hf : 32 * (hf + 1)]))
        load_w("w2", w2, 0, 0)
        load_w("w2", w2, 1, SLOT)
        load_w("w3", w3, 0, 2 * SLOT)
        load_w("w3", w3, 1, 3 * SLOT + S2)
        v2_s = big.tile([P, S2], U8, name="v2_s", offset=SLOT * 3, align_bytes=64)
        nc.vector.tensor_copy(v2_s[:], tab2_s[:].indirect(idx2[:]))

        w_c, w_s = {}, {}

        def quantise_w(name, copy):
            for a in range(PASSES):
                wb = ring.tile([P, 4 * H], BF16, name="wb", align_bytes=64)
                copy(wb[:].rearrange("p (t m j) -> p m j t", t=4, j=4),
                     w_raw[name, a][:].rearrange("p j (m t) -> p m j t", t=4))
                w_c[name, a] = kept_tile([P, H], U32, "%s_c%d" % (name, a))
                w_s[name, a] = kept_tile([P, H], U8, "%s_s%d" % (name, a))
                nc.vector.quantize_mx(w_c[name, a][:].bitcast(FP8X4), w_s[name, a][:], wb[:])

        quantise_w("w2", nc.vector.tensor_copy)
        tab2_w = big.tile([P, T3], I32, name="tab2_w", offset=0, align_bytes=64)
        nc.sync.dma_start(tab2_w[:], tab2_words[0].rearrange("p n i -> p (n i)").bitcast(I32))
        mus = []

        def load_music(g, slot):
            mus.append(big.tile([P, 4, NP], F32, name="mus%d" % g, offset=SLOT * slot, align_bytes=64))
            nc.sync.dma_start(mus[g][:], music[512 * g : 512 * (g + 1), :].rearrange("(i p) j -> p i j", p=P))

        load_music(0, 1)
        cm = [kept_tile([P, 4, HALF], F32, "cm%d" % hf) for hf in range(2)]
        for hf in range(2):
            cols = slice(HALF * hf, HALF * (hf + 1))
            for t in range(4):
                acc = psum.tile([P, HALF], F32, name="acc")
                for a in range(PASSES):
                    c0 = H * a + P * t
                    nc.tensor.matmul_mx(acc[:], w1_c[:, 2 * c0 : 2 * (c0 + P)].bitcast(FP4X4), w1_s[:, c0 : c0 + P],
                                        v_c[a, hf][:].bitcast(FP8X4), v_planes[a][:, cols],
                                        start=(a == 0), stop=(a == PASSES - 1))
                turns = ring.tile([P, HALF], F32, name="turns")
                nc.scalar.activation(turns[:], acc[:], ACT.Abs, bias=ph_turns[:, t : t + 1], scale=1.0 / TWO_PI)
                whole = ring.tile([P, HALF], U32, name="whole")
                nc.scalar.activation(whole[:], turns[:], ACT.Copy, bias=0.25)
                red = ring.tile([P, HALF], F32, name="red")
                nc.vector.scalar_tensor_tensor(red[:], whole[:].bitcast(I32), 0.25, turns[:], ALU.subtract, ALU.subtract)
                nc.scalar.activation(cm[hf][:, t, :], red[:], ACT.Sin, scale=-TWO_PI)

        quantise_w("w3", nc.scalar.copy)
        load_music(1, 2)
        for hf in range(2):
            cols = slice(HALF * hf, HALF * (hf + 1))
            for t in range(4):
                acc = psum.tile([P, HALF], F32, name="acc")
                for a in range(PASSES):
                    nc.tensor.matmul_mx(acc[:], w_c["w2", a][:, P * t : P * (t + 1)].bitcast(FP8X4),
                                        w_s["w2", a][:, P * t : P * (t + 1)],
                                        v_c[a, hf][:].bitcast(FP8X4), v_planes[a][:, cols],
                                        start=(a == 0), stop=(a == PASSES - 1))
                nc.vector.tensor_tensor(cm[hf][:, t, :], acc[:], cm[hf][:, t, :], ALU.mult)

        h_c, h_s = [], []
        for hf in range(2):
            hb = ring.tile([P, 4 * HALF], BF16, name="wb", align_bytes=64)
            for b in range(4):
                acc = psum.tile([P, 4, P], F32, name="acc")
                for t in range(4):
                    for a in range(PASSES):
                        j0 = HALF * hf + P * b
                        nc.tensor.matmul_mx(acc[:, t, :], w_c["w3", a][:, P * t : P * (t + 1)].bitcast(FP8X4),
                                            w_s["w3", a][:, P * t : P * (t + 1)],
                                            v_c[a, hf][:, P * b : P * (b + 1)].bitcast(FP8X4), v_planes[a][:, j0 : j0 + P],
                                            start=(a == 0), stop=(a == PASSES - 1))
                nc.vector.tensor_tensor(
                    hb[:, 4 * P * b : 4 * P * (b + 1)].rearrange("p (n i t) -> p n t i", i=4, t=4),
                    acc[:].rearrange("p t (n i) -> p n t i", i=4),
                    cm[hf][:, :, P * b : P * (b + 1)].rearrange("p t (n i) -> p n t i", i=4),
                    ALU.add)
            h_c.append(kept_tile([P, HALF], U32, "h_c%d" % hf))
            h_s.append(kept_tile([P, HALF], U8, "h_s%d" % hf))
            nc.vector.quantize_mx(h_c[hf][:].bitcast(FP8X4), h_s[hf][:], hb[:])

        v2_c = []
        for g in range(4):
            v2_c.append(kept_tile([P, 2 * P], U32, "v2_c%d" % g))
            nc.vector.tensor_copy(v2_c[g][:], tab2_w[:].bitcast(U32).indirect(idx2[:, 16 * g : 16 * (g + 1)]))
        for i in range(S2 // P):
            rows = slice(P * i, P * (i + 1))
            e = ring.tile([P, S], F32, name="e")
            for hf in range(2):
                acc = psum.tile([P, HALF], F32, name="acc")
                nc.tensor.matmul_mx(acc[:], v2_c[i // 2][:, P * (i % 2) : P * (i % 2 + 1)].bitcast(FP8X4), v2_s[:, rows],
                                    h_c[hf][:].bitcast(FP8X4), h_s[hf][:], start=True, stop=True)
                nc.scalar.copy(e[:, HALF * hf : HALF * (hf + 1)], acc[:])
            lead = ring.tile([P, NP], F32, name="lead")
            nc.vector.tensor_tensor(lead[:], e[:].indirect(p1[:]), mus[i // 4][:, i % 4, :], ALU.mult)
            res = ring.tile([P, NP], F32, name="res")
            nc.vector.tensor_tensor(res[:], e[:].indirect(p2[:]), lead[:], ALU.mult)
            nc.sync.dma_start(out[rows, :], res[:])
